import numpy as np
import ml_dtypes


def mxq(x, axis, fmt="e4m3"):
    dtype, down = {"e4m3": (ml_dtypes.float8_e4m3fn, 7), "e5m2": (ml_dtypes.float8_e5m2, 14)}[fmt]
    v = np.moveaxis(np.asarray(x, np.float32).astype(ml_dtypes.bfloat16).astype(np.float64), axis, -1)
    blocks = v.reshape(v.shape[:-1] + (-1, 32))
    amax = np.abs(blocks).max(-1, keepdims=True)
    byte = np.maximum(np.where(amax > 0, np.frexp(amax)[1] - 1 + 127, 0) - down, 1)
    scale = np.exp2(byte - 127.0)
    codes = (blocks / scale).astype(np.float32).astype(dtype).astype(np.float64)
    return np.moveaxis((codes * scale).reshape(v.shape), -1, axis)


WIDE = False


def mx_kscale(k):
    if not WIDE:
        return np.ones(k)
    levels = np.array([10, -10, 5, -5, 0])
    if k % 512:
        return np.exp2(np.random.permutation(np.resize(levels, k // 32))).repeat(32)
    a = np.empty((k // 512, 16))
    for p in range(k // 512):
        a[p, :8] = np.random.permutation(np.resize(levels, 8))
        for g in range(8):
            far = levels[np.abs(levels - a[p, g]) >= 10]
            a[p, g + 8] = far[np.random.randint(len(far))]
    return np.exp2(a.ravel()).repeat(32)


def f64(x):
    return np.asarray(x).astype(np.float64)


def striped(idx):
    return np.tile(idx.reshape(-1, 16).T, (8, 1)).astype(np.uint16)


def unstriped(offs):
    return offs[:16].T.reshape(-1).astype(np.int64)


def striped8(idx):
    return np.concatenate([x.reshape(-1, 16).T for x in idx]).astype(np.uint16)


def runs(offs, k):
    lists = np.stack([offs[16 * r : 16 * r + 16].T.reshape(-1) for r in range(8)]).astype(np.int64)
    return lists[np.arange(k) % 512 // 64]


def pack_weight(w):
    k, n = w.shape
    w = f64(np.asarray(w, np.float32).astype(ml_dtypes.bfloat16)).reshape(k // 32, 32, n)
    amax = np.abs(w).max(1)
    byte = np.clip(np.where(amax > 0, np.frexp(amax)[1] - 1 + 127 - 7, 1), 1, 254)
    scaled = (w * np.exp2(127.0 - byte)[:, None, :]).reshape(k, n).astype(np.float32)
    words = np.ascontiguousarray(scaled.reshape(k // 512, 128, 4, n).transpose(0, 1, 3, 2)).astype(ml_dtypes.float8_e4m3fn).view(np.uint8)
    return words, np.ascontiguousarray(byte.astype(np.uint8).reshape(k // 512, 16, n))


def unpack_weight(words, scales):
    g, p, n, _ = words.shape
    vals = np.ascontiguousarray(words).view(ml_dtypes.float8_e4m3fn).astype(np.float64) * np.repeat(np.exp2(scales.astype(np.float64) - 127.0), 8, axis=1)[..., None]
    return vals.transpose(0, 1, 3, 2).reshape(g * 512, n)


def sigmoid(v):
    return 1.0 / (1.0 + np.exp(-np.maximum(v, -700.0)))


K, T, S, N, H = 512, 2048, 512, 512, 512


def setup_inputs():
    n = np.random.standard_normal
    s = mx_kscale(K)[:, None]
    u = mx_kscale(S)
    packed_xT = pack_weight(n((K, T)) * s)
    return {
        "x_words": packed_xT[0],
        "x_scales": packed_xT[1],
        "wa": (n((K, H)) / np.sqrt(K) / s).astype(np.float32),
        "wb": (n((K, N)) / np.sqrt(K) / s).astype(np.float32),
        "gt": (np.random.uniform(0.5, 1.5, (S, 1)) * u[:, None]).astype(np.float32),
        "gi": (np.random.uniform(0.5, 1.5, (S, 1)) / u[:, None]).astype(np.float32),
        "offs": striped(np.random.permutation(T)[:S]),
        "two": striped(np.random.permutation(T)[:S]),
        "n1": striped8(np.stack([np.random.permutation(H) for _ in range(8)])),
        "n2": striped8(np.stack([np.random.permutation(H) for _ in range(8)])),
        "n3": striped8(np.stack([np.random.permutation(H) for _ in range(8)])),
        "n4": striped8(np.stack([np.random.permutation(N) for _ in range(8)])),
        "n5": striped8(np.stack([np.random.permutation(N) for _ in range(8)])),
    }


def reference(x_words, x_scales, wa, wb, gt, gi, offs, two, n1, n2, n3, n4, n5):
    xq = unpack_weight(x_words, x_scales)[:, unstriped(offs)]
    a = xq.T @ mxq(f64(wa), 0, "e4m3")
    b1 = a[np.arange(S)[:, None], runs(n1, S)]
    b2 = a[np.arange(S)[:, None], runs(n2, S)]
    b3 = a[np.arange(S)[:, None], runs(n3, S)]
    z = f64(gt) * (np.maximum(np.maximum(b1, b2), b3) - (0.5 * (np.maximum(np.minimum(b1, b2), np.minimum(np.maximum(b1, b2), b3)))))
    x_two = unpack_weight(x_words, x_scales)[:, unstriped(two)]
    b = x_two.T @ mxq(f64(wb), 0, "e4m3")
    z2 = f64(gi) * b
    cv = 0.0625 * ((mxq(z, 0, "e4m3").T @ mxq(z2, 0, "e4m3")))
    sm = np.maximum(cv, cv[np.arange(H)[:, None], runs(n5, H)])
    ds = np.zeros((H, N))
    ds[np.arange(H)[:, None], runs(n4, H)] = sm
    return ds * sigmoid(cv)

@@ -1,0 +1,215 @@
+from contextlib import ExitStack
+
+import concourse.mybir as mybir
+from concourse.masks import make_identity
+
+K, T, S, H, N = 512, 2048, 512, 512, 512
+FLOPS = 2 * K * S * H + 2 * K * S * N + 2 * S * H * N
+
+F32 = mybir.dt.float32
+BF16 = mybir.dt.bfloat16
+I32 = mybir.dt.int32
+U32 = mybir.dt.uint32
+U16 = mybir.dt.uint16
+U8 = mybir.dt.uint8
+FP8X4 = mybir.dt.float8_e4m3fn_x4
+ALU = mybir.AluOpType
+ACT = mybir.ActivationFunctionType
+
+P = 128
+PACK = 4
+WIN = 1024
+
+
+def tile_picked_momtop2sendg_none_p_kernel(tc, x_words, x_scales, wa, wb, gt, gi, offs, two, n1, n2, n3, n4, n5, out):
+    nc = tc.nc
+    with ExitStack() as ctx:
+        sb = ctx.enter_context(tc.tile_pool(name="sb", bufs=1))
+        ps = ctx.enter_context(tc.psum_pool(name="ps", bufs=1))
+
+        def tile(shape, dtype, name):
+            return sb.tile(shape, dtype, name=name, align_bytes=64)
+
+        def load_list(src, name):
+            dst = tile([P, S // 16], U16, name)
+            nc.sync.dma_start(dst[:], src)
+            return dst
+
+        warm = tile([P, 1], F32, "warm")
+        nc.gpsimd.memset(warm[:], 0.0)
+        warm_out = tile([P, 1], F32, "warm_out")
+        nc.scalar.activation(warm_out[:], warm[:], ACT.Sigmoid)
+
+        xs = tile([P, T], U8, "xs")
+        nc.vector.memset(xs[:].bitcast(I32), 0)
+        offs_l = load_list(offs, "offs_l")
+        two_l = load_list(two, "two_l")
+        for q in range(4):
+            nc.sync.dma_start(xs[32 * q : 32 * q + 4, :].bitcast(I32), x_scales[0, 4 * q : 4 * q + 4, :].bitcast(I32))
+        wa_raw = tile([P, PACK, H], F32, "wa_raw")
+        nc.sync.dma_start(wa_raw[:], wa.rearrange("(p j) n -> p j n", j=PACK))
+        xw = tile([P, T], I32, "xw")
+        nc.sync.dma_start(xw[:], x_words[0].rearrange("p c r -> p (c r)").bitcast(I32))
+        g_rows = tile([P, P], F32, "g_rows")
+        nc.gpsimd.memset(g_rows[:], 0.0)
+        for row0, vec in ((0, gt), (PACK, gi)):
+            nc.gpsimd.dma_start(
+                g_rows[row0 : row0 + PACK, :].rearrange("t (q e) -> t q e", e=8),
+                vec.rearrange("(q t e) o -> t q (e o)", t=PACK, e=8),
+            )
+        ident = tile([P, P], F32, "ident")
+        make_identity(nc, ident[:])
+        g_bank = ps.tile([P, P], F32, name="g_bank", tag="hi0")
+        nc.tensor.transpose(g_bank[:], g_rows[:], ident[:])
+        g_cols = tile([P, 2 * PACK], F32, "g_cols")
+        nc.scalar.copy(g_cols[:], g_bank[:, 0 : 2 * PACK])
+        n1_l = load_list(n1, "n1_l")
+        n2_l = load_list(n2, "n2_l")
+        n3_l = load_list(n3, "n3_l")
+        wb_raw = tile([P, PACK, N], F32, "wb_raw")
+        nc.sync.dma_start(wb_raw[:], wb.rearrange("(p j) n -> p j n", j=PACK))
+        n5_l = load_list(n5, "n5_l")
+        n4_l = load_list(n4, "n4_l")
+
+        half_gt = tile([P, PACK], F32, "half_gt")
+        nc.scalar.activation(half_gt[:], g_cols[:, 0:PACK], ACT.Abs, scale=0.5)
+        sign_gt = tile([P, PACK], F32, "sign_gt")
+        nc.gpsimd.tensor_scalar(sign_gt[:], g_cols[:, 0:PACK], 0.0, 2.0, ALU.is_ge, ALU.mult)
+        sign1 = tile([P, PACK], F32, "sign1")
+        nc.gpsimd.tensor_scalar(sign1[:], sign_gt[:], 1.0, -1.0, ALU.mult, ALU.add)
+        signed_gi = tile([P, PACK], F32, "signed_gi")
+        nc.gpsimd.tensor_tensor(signed_gi[:], sign1[:], g_cols[:, PACK : 2 * PACK], ALU.mult)
+
+        def pick_scales(lst, name):
+            plain = tile([P, S], U8, name + "_plain")
+            nc.vector.tensor_copy(plain[:], xs[:].indirect(lst[:]))
+            dealt = tile([P, S], U8, name)
+            nc.vector.tensor_copy(
+                dealt[:].bitcast(I32).rearrange("p (t q e) -> p q t e", t=PACK, e=2),
+                plain[:].bitcast(I32).rearrange("p (q t e) -> p q t e", t=PACK, e=2),
+            )
+            return dealt
+
+        def pick_words(lst, name):
+            dealt = tile([P, S], I32, name)
+            nc.vector.tensor_copy(
+                dealt[:].bitcast(U32).rearrange("p (t q e) -> p q t e", t=PACK, e=8),
+                xw[:].bitcast(U32).indirect(lst[:]),
+            )
+            return dealt
+
+        def interleave(engine_copy, grouped, raw, c0, c1):
+            engine_copy(
+                grouped[:, c0:c1, :].rearrange("p (c i) j -> p c j i", i=4),
+                raw[:, :, c0:c1].rearrange("p j (c i) -> p c j i", i=4),
+            )
+
+        def quantize(grouped, name):
+            width = grouped.shape[1]
+            codes = tile([P, width], I32, name + "_codes")
+            scales = tile([P, width], U8, name + "_scales")
+            nc.vector.quantize_mx(codes[:].bitcast(FP8X4), scales[:], grouped[:].rearrange("p c j -> p (c j)"))
+            return codes, scales
+
+        def product(bank, lhs, t, rhs):
+            cols = slice(P * t, P * (t + 1))
+            nc.tensor.matmul_mx(
+                bank[:], lhsT=lhs[0][:, cols].bitcast(FP8X4), lhsT_scale=lhs[1][:, cols],
+                rhs=rhs[0][:].bitcast(FP8X4), rhs_scale=rhs[1][:], start=True, stop=True,
+            )
+
+        xa_scales = pick_scales(offs_l, "xa_scales")
+        xb_scales = pick_scales(two_l, "xb_scales")
+        wa_g = tile([P, H, PACK], BF16, "wa_g")
+        interleave(nc.scalar.copy, wa_g, wa_raw, 0, 128)
+        interleave(nc.scalar.copy, wa_g, wa_raw, 128, 256)
+        interleave(nc.vector.tensor_copy, wa_g, wa_raw, 256, 512)
+        wa_q = quantize(wa_g, "wa")
+        xa = (pick_words(offs_l, "xa_words"), xa_scales)
+        xb = (pick_words(two_l, "xb_words"), xb_scales)
+
+        a_win = []
+        for t in range(PACK):
+            bank = ps.tile([P, H], F32, name="a_bank%d" % t, tag="lo%d" % t)
+            product(bank, xa, t, wa_q)
+            win = tile([P, WIN], F32, "a_win%d" % t)
+            nc.scalar.activation(win[:, 0:H], bank[:], ACT.Copy, scale=half_gt[:, t : t + 1])
+            a_win.append(win)
+
+        wb_g = tile([P, N, PACK], BF16, "wb_g")
+        for c in range(4):
+            interleave(nc.scalar.copy, wb_g, wb_raw, 128 * c, 128 * (c + 1))
+
+        hi = tile([P, PACK, H], F32, "hi")
+        rest = tile([P, PACK, H], F32, "rest")
+        b1 = [tile([P, H], F32, "b1_%d" % t) for t in range(PACK)]
+        d = [tile([P, H], F32, "d_%d" % t) for t in range(PACK)]
+        gap = [tile([P, H], F32, "gap_%d" % t) for t in range(PACK)]
+        e = [tile([P, H], F32, "e_%d" % t) for t in range(PACK)]
+        w = [tile([P, H], F32, "w_%d" % t) for t in range(PACK)]
+
+        def top_two(pair):
+            for t in pair:
+                nc.vector.tensor_copy(b1[t][:], a_win[t][:].indirect(n1_l[:]))
+            for t in pair:
+                nc.vector.tensor_tensor(d[t][:], a_win[t][:].indirect(n2_l[:]), b1[t][:], ALU.subtract)
+                nc.scalar.activation(gap[t][:], d[t][:], ACT.Abs)
+            for t in pair:
+                nc.vector.scalar_tensor_tensor(hi[:, t, :], d[t][:], 0.0, b1[t][:], ALU.max, ALU.add)
+            for t in pair:
+                nc.vector.tensor_tensor(e[t][:], a_win[t][:].indirect(n3_l[:]), hi[:, t, :], ALU.subtract)
+            for t in pair:
+                nc.vector.scalar_tensor_tensor(w[t][:], e[t][:], -1.0, gap[t][:], ALU.mult, ALU.min)
+            for t in pair:
+                nc.vector.scalar_tensor_tensor(rest[:, t, :], e[t][:], 2.0, w[t][:], ALU.mult, ALU.max)
+
+        top_two((0, 1))
+        wb_q = quantize(wb_g, "wb")
+        z2_raw = tile([P, PACK, N], BF16, "z2_raw")
+        for t in range(PACK):
+            bank = ps.tile([P, N], F32, name="b_bank%d" % t, tag="hi%d" % t)
+            product(bank, xb, t, wb_q)
+            nc.scalar.activation(z2_raw[:, t, :], bank[:], ACT.Copy, scale=signed_gi[:, t : t + 1])
+        z2_g = tile([P, N, PACK], BF16, "z2_g")
+        for c in range(4):
+            interleave(nc.scalar.copy, z2_g, z2_raw, 128 * c, 128 * (c + 1))
+        top_two((2, 3))
+        z2_q = quantize(z2_g, "z2")
+
+        hi_v = hi[:].rearrange("p t (c s i) -> p s c t i", s=PACK, i=2)
+        rest_v = rest[:].rearrange("p t (c s i) -> p s c t i", s=PACK, i=2)
+        z_g = [tile([P, P, PACK], BF16, "z_g%d" % s) for s in range(PACK)]
+        z_q = []
+        for s in range(PACK + 1):
+            if s < PACK:
+                nc.vector.tensor_tensor(z_g[s][:].rearrange("p (c i) t -> p c t i", i=2), hi_v[:, s], rest_v[:, s], ALU.add)
+            if s > 0:
+                z_q.append(quantize(z_g[s - 1], "zs%d" % (s - 1)))
+
+        out_v = out.rearrange("(c s i) n -> s c i n", s=PACK, i=2)
+        banks, cv_win, sig = [], [], []
+        for s in range(PACK):
+            bank = ps.tile([P, N], F32, name="cv_bank%d" % s, tag="lo%d" % s)
+            product(bank, z_q[s], 0, z2_q)
+            win = tile([P, WIN], F32, "cv_win%d" % s)
+            nc.scalar.activation(win[:, 0:N], bank[:], ACT.Copy, scale=0.0625)
+            banks.append(bank)
+            cv_win.append(win)
+        for s in range(PACK):
+            sg = tile([P, N], F32, "sig%d" % s)
+            nc.scalar.activation(sg[:], banks[s][:], ACT.Sigmoid, scale=0.0625)
+            sig.append(sg)
+        other = [tile([P, N], F32, "other%d" % s) for s in range(PACK)]
+        sm = [tile([P, N], F32, "sm%d" % s) for s in range(PACK)]
+        for s in range(PACK + 1):
+            if s < PACK:
+                nc.vector.tensor_copy(other[s][:], cv_win[s][:].indirect(n5_l[:]))
+            if s > 0:
+                nc.vector.scalar_tensor_tensor(sm[s - 1][:], banks[s - 1][:], 0.0625, other[s - 1][:], ALU.mult, ALU.max)
+        for s in range(PACK):
+            ds = tile([P, WIN], F32, "ds%d" % s)
+            nc.vector.tensor_copy(ds[:].indirect(n4_l[:]), sm[s][:])
+            res = tile([P, N], F32, "res%d" % s)
+            engine = nc.vector if s == PACK - 1 else nc.gpsimd
+            engine.tensor_tensor(res[:], ds[:, 0:N], sig[s][:], ALU.mult)
+            nc.sync.dma_start(out_v[s], res[:])

@@ -18,198 +18,281 @@ ACT = mybir.ActivationFunctionType
 
 P = 128
 PACK = 4
-WIN = 1024
+RUN = 8
+QUADRANT = 32
+GROUP = 16
+LINE = 4
+WINDOW = 1024
+PIECE = 128
+CV_SCALE = 0.0625
+LAST = PACK - 1
+TENSOR_TILES = (0, 1)
+VECTOR_TILES = (2, 3)
 
 
-def tile_picked_momtop2sendg_none_p_kernel(tc, x_words, x_scales, wa, wb, gt, gi, offs, two, n1, n2, n3, n4, n5, out):
+def tile_picked_momtop2sendg_none_p_kernel(
+    tc, x_words, x_scales, wa, wb, gt, gi, offs, two, n1, n2, n3, n4, n5, out
+):
     nc = tc.nc
     with ExitStack() as ctx:
         sb = ctx.enter_context(tc.tile_pool(name="sb", bufs=1))
         ps = ctx.enter_context(tc.psum_pool(name="ps", bufs=1))
 
-        def tile(shape, dtype, name):
-            return sb.tile(shape, dtype, name=name, align_bytes=64)
+        def tile(shape, dtype, name, on=None):
+            return sb.tile(shape, dtype, name=name, tag=on or name, align_bytes=64)
+
+        def bank(width, name, number):
+            return ps.tile([P, width], F32, name=name, tag="bank%d" % number)
 
         def load_list(src, name):
-            dst = tile([P, S // 16], U16, name)
+            dst = tile([P, S // GROUP], U16, name)
             nc.sync.dma_start(dst[:], src)
             return dst
 
-        warm = tile([P, 1], F32, "warm")
-        nc.gpsimd.memset(warm[:], 0.0)
-        warm_out = tile([P, 1], F32, "warm_out")
-        nc.scalar.activation(warm_out[:], warm[:], ACT.Sigmoid)
-
-        xs = tile([P, T], U8, "xs")
-        nc.vector.memset(xs[:].bitcast(I32), 0)
-        offs_l = load_list(offs, "offs_l")
-        two_l = load_list(two, "two_l")
-        for q in range(4):
-            nc.sync.dma_start(xs[32 * q : 32 * q + 4, :].bitcast(I32), x_scales[0, 4 * q : 4 * q + 4, :].bitcast(I32))
-        wa_raw = tile([P, PACK, H], F32, "wa_raw")
-        nc.sync.dma_start(wa_raw[:], wa.rearrange("(p j) n -> p j n", j=PACK))
-        xw = tile([P, T], I32, "xw")
-        nc.sync.dma_start(xw[:], x_words[0].rearrange("p c r -> p (c r)").bitcast(I32))
-        g_rows = tile([P, P], F32, "g_rows")
-        nc.gpsimd.memset(g_rows[:], 0.0)
-        for row0, vec in ((0, gt), (PACK, gi)):
-            nc.gpsimd.dma_start(
-                g_rows[row0 : row0 + PACK, :].rearrange("t (q e) -> t q e", e=8),
-                vec.rearrange("(q t e) o -> t q (e o)", t=PACK, e=8),
+        def load_factor(vec, name):
+            rows = tile([P, P], F32, name)
+            nc.vector.memset(rows[:], 0.0)
+            nc.sync.dma_start(
+                rows[0:PACK, :].rearrange("t (g e) -> t g e", e=RUN),
+                vec.rearrange("(g t e) o -> t g (e o)", t=PACK, e=RUN),
             )
+            return rows
+
+        def load_weight(cols, name):
+            raw = tile([P, PACK, cols.shape[1]], F32, name)
+            nc.sync.dma_start(raw[:], cols.rearrange("(p j) n -> p j n", j=PACK))
+            return raw
+
+        zero = tile([P, 1], F32, "zero")
+        nc.gpsimd.memset(zero[:], 0.0)
+        half = tile([P, 1], F32, "half")
+        nc.scalar.activation(half[:], zero[:], ACT.Sigmoid)
         ident = tile([P, P], F32, "ident")
         make_identity(nc, ident[:])
-        g_bank = ps.tile([P, P], F32, name="g_bank", tag="hi0")
-        nc.tensor.transpose(g_bank[:], g_rows[:], ident[:])
-        g_cols = tile([P, 2 * PACK], F32, "g_cols")
-        nc.scalar.copy(g_cols[:], g_bank[:, 0 : 2 * PACK])
+
+        offs_l = load_list(offs, "offs_l")
+        words = tile([P, T], I32, "words")
+        nc.sync.dma_start(words[:], x_words[0].rearrange("p c r -> p (c r)").bitcast(I32))
+        two_l = load_list(two, "two_l")
+        gt_rows = load_factor(gt, "gt_rows")
+        scales = tile([P, T], U8, "scales")
+        nc.vector.memset(scales[:].bitcast(I32), 0)
+        for q in range(P // QUADRANT):
+            nc.sync.dma_start(
+                scales[QUADRANT * q : QUADRANT * q + PACK, :].bitcast(I32),
+                x_scales[0, PACK * q : PACK * (q + 1), :].bitcast(I32),
+            )
+        halves = [slice(0, H // 2), slice(H // 2, H)]
+        wa_raw = [load_weight(wa[:, cols], "wa_raw%d" % h) for h, cols in enumerate(halves)]
         n1_l = load_list(n1, "n1_l")
         n2_l = load_list(n2, "n2_l")
         n3_l = load_list(n3, "n3_l")
-        wb_raw = tile([P, PACK, N], F32, "wb_raw")
-        nc.sync.dma_start(wb_raw[:], wb.rearrange("(p j) n -> p j n", j=PACK))
+        gi_rows = load_factor(gi, "gi_rows")
+        wb_raw = load_weight(wb, "wb_raw")
         n5_l = load_list(n5, "n5_l")
         n4_l = load_list(n4, "n4_l")
 
-        half_gt = tile([P, PACK], F32, "half_gt")
-        nc.scalar.activation(half_gt[:], g_cols[:, 0:PACK], ACT.Abs, scale=0.5)
-        sign_gt = tile([P, PACK], F32, "sign_gt")
-        nc.gpsimd.tensor_scalar(sign_gt[:], g_cols[:, 0:PACK], 0.0, 2.0, ALU.is_ge, ALU.mult)
-        sign1 = tile([P, PACK], F32, "sign1")
-        nc.gpsimd.tensor_scalar(sign1[:], sign_gt[:], 1.0, -1.0, ALU.mult, ALU.add)
-        signed_gi = tile([P, PACK], F32, "signed_gi")
-        nc.gpsimd.tensor_tensor(signed_gi[:], sign1[:], g_cols[:, PACK : 2 * PACK], ALU.mult)
+        def turn_factor(rows, name, number):
+            turned_rows = bank(P, name, number)
+            nc.tensor.transpose(turned_rows[:], rows[:], ident[:])
+            return turned_rows[:, 0:PACK]
 
-        def pick_scales(lst, name):
-            plain = tile([P, S], U8, name + "_plain")
-            nc.vector.tensor_copy(plain[:], xs[:].indirect(lst[:]))
-            dealt = tile([P, S], U8, name)
-            nc.vector.tensor_copy(
-                dealt[:].bitcast(I32).rearrange("p (t q e) -> p q t e", t=PACK, e=2),
-                plain[:].bitcast(I32).rearrange("p (q t e) -> p q t e", t=PACK, e=2),
-            )
-            return dealt
+        gt_cols = turn_factor(gt_rows, "gt_cols", 4)
+        half_gt = tile([P, PACK], F32, "half_gt")
+        nc.scalar.activation(half_gt[:], gt_cols, ACT.Abs, scale=0.5)
+        sign_or_zero = tile([P, PACK], F32, "sign_or_zero")
+        nc.scalar.activation(sign_or_zero[:], gt_cols, ACT.Sign)
+        sign_gt = tile([P, PACK], F32, "sign_gt")
+        nc.scalar.activation(sign_gt[:], sign_or_zero[:], ACT.Sign, bias=half[:])
 
         def pick_words(lst, name):
             dealt = tile([P, S], I32, name)
             nc.vector.tensor_copy(
-                dealt[:].bitcast(U32).rearrange("p (t q e) -> p q t e", t=PACK, e=8),
-                xw[:].bitcast(U32).indirect(lst[:]),
+                dealt[:].bitcast(U32).rearrange("p (t g e) -> p g t e", t=PACK, e=RUN),
+                words[:].bitcast(U32).indirect(lst[:]),
             )
             return dealt
 
-        def interleave(engine_copy, grouped, raw, c0, c1):
-            engine_copy(
-                grouped[:, c0:c1, :].rearrange("p (c i) j -> p c j i", i=4),
-                raw[:, :, c0:c1].rearrange("p j (c i) -> p c j i", i=4),
+        def pick_scales(lst, name, on=None):
+            plain = tile([P, S], U8, name + "_plain", on)
+            nc.vector.tensor_copy(plain[:], scales[:].indirect(lst[:]))
+            dealt = tile([P, S], U8, name)
+            nc.vector.tensor_copy(
+                dealt[:].bitcast(I32).rearrange("p (t g e) -> p g t e", t=PACK, e=RUN // 4),
+                plain[:].bitcast(I32).rearrange("p (g t e) -> p g t e", t=PACK, e=RUN // 4),
+            )
+            return dealt
+
+        def interleave(grouped, raw):
+            for c0 in range(0, raw.shape[2], PIECE):
+                nc.scalar.copy(
+                    grouped[:, c0 : c0 + PIECE, :].rearrange("p (c i) j -> p c j i", i=LINE),
+                    raw[:, :, c0 : c0 + PIECE].rearrange("p j (c i) -> p c j i", i=LINE),
+                )
+
+        def packed(width, name):
+            return tile([P, width], I32, name + "_codes"), tile([P, width], U8, name + "_scales")
+
+        def quantize(operand, cols, grouped):
+            nc.vector.quantize_mx(
+                operand[0][:, cols].bitcast(FP8X4), operand[1][:, cols], grouped[:].rearrange("p c j -> p (c j)")
             )
 
-        def quantize(grouped, name):
-            width = grouped.shape[1]
-            codes = tile([P, width], I32, name + "_codes")
-            scales = tile([P, width], U8, name + "_scales")
-            nc.vector.quantize_mx(codes[:].bitcast(FP8X4), scales[:], grouped[:].rearrange("p c j -> p (c j)"))
-            return codes, scales
-
-        def product(bank, lhs, t, rhs):
-            cols = slice(P * t, P * (t + 1))
+        def product(result, lhs, t, rhs, cols):
+            lhs_cols = slice(P * t, P * (t + 1))
             nc.tensor.matmul_mx(
-                bank[:], lhsT=lhs[0][:, cols].bitcast(FP8X4), lhsT_scale=lhs[1][:, cols],
-                rhs=rhs[0][:].bitcast(FP8X4), rhs_scale=rhs[1][:], start=True, stop=True,
+                result[:],
+                lhsT=lhs[0][:, lhs_cols].bitcast(FP8X4),
+                lhsT_scale=lhs[1][:, lhs_cols],
+                rhs=rhs[0][:, cols].bitcast(FP8X4),
+                rhs_scale=rhs[1][:, cols],
+                start=True,
+                stop=True,
             )
 
-        xa_scales = pick_scales(offs_l, "xa_scales")
-        xb_scales = pick_scales(two_l, "xb_scales")
-        wa_g = tile([P, H, PACK], BF16, "wa_g")
-        interleave(nc.scalar.copy, wa_g, wa_raw, 0, 128)
-        interleave(nc.scalar.copy, wa_g, wa_raw, 128, 256)
-        interleave(nc.vector.tensor_copy, wa_g, wa_raw, 256, 512)
-        wa_q = quantize(wa_g, "wa")
-        xa = (pick_words(offs_l, "xa_words"), xa_scales)
-        xb = (pick_words(two_l, "xb_words"), xb_scales)
+        every = slice(0, N)
+        xa_words = pick_words(offs_l, "xa_words")
+        xb_words = pick_words(two_l, "xb_words")
+        xa = (xa_words, pick_scales(offs_l, "xa_scales"))
+        wa_q = packed(H, "wa")
+        a_win = [tile([P, WINDOW], F32, "a_win%d" % t) for t in range(PACK)]
+        for h, cols in enumerate(halves):
+            wa_grouped = tile([P, H // 2, PACK], BF16, "wa_grouped%d" % h)
+            interleave(wa_grouped, wa_raw[h])
+            quantize(wa_q, cols, wa_grouped)
+            a_half = bank(H // 2, "a_half%d" % h, 6 + h)
+            product(a_half, xa, 0, wa_q, cols)
+            nc.scalar.activation(a_win[0][:, cols], a_half[:], ACT.Copy, scale=half_gt[:, 0:1])
+        xb = (xb_words, pick_scales(two_l, "xb_scales", on="wa_grouped1"))
+        for t in range(1, PACK):
+            a_bank = bank(H, "a_bank%d" % t, t)
+            product(a_bank, xa, t, wa_q, every)
+            nc.scalar.activation(a_win[t][:, 0:H], a_bank[:], ACT.Copy, scale=half_gt[:, t : t + 1])
 
-        a_win = []
-        for t in range(PACK):
-            bank = ps.tile([P, H], F32, name="a_bank%d" % t, tag="lo%d" % t)
-            product(bank, xa, t, wa_q)
-            win = tile([P, WIN], F32, "a_win%d" % t)
-            nc.scalar.activation(win[:, 0:H], bank[:], ACT.Copy, scale=half_gt[:, t : t + 1])
-            a_win.append(win)
-
-        wb_g = tile([P, N, PACK], BF16, "wb_g")
-        for c in range(4):
-            interleave(nc.scalar.copy, wb_g, wb_raw, 128 * c, 128 * (c + 1))
+        gi_cols = turn_factor(gi_rows, "gi_cols", 5)
+        signed_gi = tile([P, PACK], F32, "signed_gi")
+        nc.vector.tensor_tensor(signed_gi[:], gi_cols, sign_gt[:], ALU.mult)
+        wb_grouped = tile([P, N, PACK], BF16, "wb_grouped")
+        interleave(wb_grouped, wb_raw)
 
         hi = tile([P, PACK, H], F32, "hi")
         rest = tile([P, PACK, H], F32, "rest")
         b1 = [tile([P, H], F32, "b1_%d" % t) for t in range(PACK)]
-        d = [tile([P, H], F32, "d_%d" % t) for t in range(PACK)]
+        diff = [tile([P, H], F32, "diff_%d" % t) for t in range(PACK)]
         gap = [tile([P, H], F32, "gap_%d" % t) for t in range(PACK)]
-        e = [tile([P, H], F32, "e_%d" % t) for t in range(PACK)]
-        w = [tile([P, H], F32, "w_%d" % t) for t in range(PACK)]
+        over = [tile([P, H], F32, "over_%d" % t) for t in range(PACK)]
+        under = [tile([P, H], F32, "under_%d" % t) for t in range(PACK)]
 
-        def top_two(pair):
+        def look_up(pair):
             for t in pair:
                 nc.vector.tensor_copy(b1[t][:], a_win[t][:].indirect(n1_l[:]))
             for t in pair:
-                nc.vector.tensor_tensor(d[t][:], a_win[t][:].indirect(n2_l[:]), b1[t][:], ALU.subtract)
-                nc.scalar.activation(gap[t][:], d[t][:], ACT.Abs)
+                nc.vector.tensor_tensor(diff[t][:], a_win[t][:].indirect(n2_l[:]), b1[t][:], ALU.subtract)
+                nc.scalar.activation(gap[t][:], diff[t][:], ACT.Abs)
             for t in pair:
-                nc.vector.scalar_tensor_tensor(hi[:, t, :], d[t][:], 0.0, b1[t][:], ALU.max, ALU.add)
+                nc.vector.scalar_tensor_tensor(hi[:, t, :], diff[t][:], 0.0, b1[t][:], ALU.max, ALU.add)
             for t in pair:
-                nc.vector.tensor_tensor(e[t][:], a_win[t][:].indirect(n3_l[:]), hi[:, t, :], ALU.subtract)
+                nc.vector.tensor_tensor(over[t][:], a_win[t][:].indirect(n3_l[:]), hi[:, t, :], ALU.subtract)
             for t in pair:
-                nc.vector.scalar_tensor_tensor(w[t][:], e[t][:], -1.0, gap[t][:], ALU.mult, ALU.min)
-            for t in pair:
-                nc.vector.scalar_tensor_tensor(rest[:, t, :], e[t][:], 2.0, w[t][:], ALU.mult, ALU.max)
+                nc.vector.scalar_tensor_tensor(under[t][:], over[t][:], -1.0, gap[t][:], ALU.mult, ALU.min)
 
-        top_two((0, 1))
-        wb_q = quantize(wb_g, "wb")
-        z2_raw = tile([P, PACK, N], BF16, "z2_raw")
+        z_rows = tile([P, PACK, H], BF16, "z_rows")
+
+        def sum_turned(pair):
+            up = {t: tile([P, H], F32, "up_%d" % t) for t in pair}
+            down = {t: tile([P, H], F32, "down_%d" % t) for t in pair}
+            for t in pair:
+                nc.scalar.activation(up[t][:], over[t][:], ACT.Relu, scale=2.0)
+            for t in pair:
+                nc.scalar.activation(down[t][:], under[t][:], ACT.Relu)
+            sums = {}
+            for t in pair:
+                sum_bank = bank(H, "sum_bank%d" % t, t)
+                for c0 in range(0, H, P):
+                    cols = slice(c0, c0 + P)
+                    terms = (hi[:, t, cols], up[t][:, cols], down[t][:, cols])
+                    for i, term in enumerate(terms):
+                        nc.tensor.matmul(
+                            sum_bank[:, cols], term, ident[:], is_transpose=True, start=i == 0, stop=i == len(terms) - 1
+                        )
+                sums[t] = tile([P, H], F32, "sum_%d" % t)
+                nc.scalar.copy(sums[t][:], sum_bank[:])
+            return sums
+
+        def turn_back(sums):
+            for t in sums:
+                back_bank = bank(H, "back_bank%d" % t, t + len(sums))
+                for c0 in range(0, H, P):
+                    cols = slice(c0, c0 + P)
+                    nc.tensor.transpose(back_bank[:, cols], sums[t][:, cols], ident[:])
+                nc.scalar.copy(z_rows[:, t, :], back_bank[:])
+
+        def sum_plain(pair):
+            for t in pair:
+                nc.vector.scalar_tensor_tensor(rest[:, t, :], over[t][:], 2.0, under[t][:], ALU.mult, ALU.max)
+            for t in pair:
+                nc.vector.tensor_tensor(z_rows[:, t, :], hi[:, t, :], rest[:, t, :], ALU.add)
+
+        look_up(TENSOR_TILES)
+        turned_sums = sum_turned(TENSOR_TILES)
+        wb_q = packed(N, "wb")
+        quantize(wb_q, every, wb_grouped)
+        z2_rows = tile([P, PACK, N], BF16, "z2_rows")
         for t in range(PACK):
-            bank = ps.tile([P, N], F32, name="b_bank%d" % t, tag="hi%d" % t)
-            product(bank, xb, t, wb_q)
-            nc.scalar.activation(z2_raw[:, t, :], bank[:], ACT.Copy, scale=signed_gi[:, t : t + 1])
-        z2_g = tile([P, N, PACK], BF16, "z2_g")
-        for c in range(4):
-            interleave(nc.scalar.copy, z2_g, z2_raw, 128 * c, 128 * (c + 1))
-        top_two((2, 3))
-        z2_q = quantize(z2_g, "z2")
+            b_bank = bank(N, "b_bank%d" % t, PACK + t)
+            product(b_bank, xb, t, wb_q, every)
+            nc.scalar.activation(z2_rows[:, t, :], b_bank[:], ACT.Copy, scale=signed_gi[:, t : t + 1])
+        look_up(VECTOR_TILES)
+        turn_back(turned_sums)
+        z2_grouped = tile([P, N, PACK], BF16, "z2_grouped")
+        interleave(z2_grouped, z2_rows)
+        z2_q = packed(N, "z2")
+        quantize(z2_q, every, z2_grouped)
+        sum_plain(VECTOR_TILES)
 
-        hi_v = hi[:].rearrange("p t (c s i) -> p s c t i", s=PACK, i=2)
-        rest_v = rest[:].rearrange("p t (c s i) -> p s c t i", s=PACK, i=2)
-        z_g = [tile([P, P, PACK], BF16, "z_g%d" % s) for s in range(PACK)]
+        z_dealt = z_rows[:].rearrange("p t (c s i) -> p s c t i", s=PACK, i=LINE)
+        z_grouped = [tile([P, P, PACK], BF16, "z_grouped%d" % s) for s in range(PACK)]
+        for s in range(PACK):
+            copy = nc.scalar.copy if s % 2 else nc.vector.tensor_copy
+            copy(z_grouped[s][:].rearrange("p (c i) t -> p c t i", i=LINE), z_dealt[:, s])
         z_q = []
-        for s in range(PACK + 1):
-            if s < PACK:
-                nc.vector.tensor_tensor(z_g[s][:].rearrange("p (c i) t -> p c t i", i=2), hi_v[:, s], rest_v[:, s], ALU.add)
-            if s > 0:
-                z_q.append(quantize(z_g[s - 1], "zs%d" % (s - 1)))
+        for s in range(PACK):
+            z_q.append(packed(P, "z_tile%d" % s))
+            quantize(z_q[s], slice(0, P), z_grouped[s])
 
-        out_v = out.rearrange("(c s i) n -> s c i n", s=PACK, i=2)
-        banks, cv_win, sig = [], [], []
+        cv_banks, cv_win, cv = [], [], {}
         for s in range(PACK):
-            bank = ps.tile([P, N], F32, name="cv_bank%d" % s, tag="lo%d" % s)
-            product(bank, z_q[s], 0, z2_q)
-            win = tile([P, WIN], F32, "cv_win%d" % s)
-            nc.scalar.activation(win[:, 0:N], bank[:], ACT.Copy, scale=0.0625)
-            banks.append(bank)
-            cv_win.append(win)
-        for s in range(PACK):
-            sg = tile([P, N], F32, "sig%d" % s)
-            nc.scalar.activation(sg[:], banks[s][:], ACT.Sigmoid, scale=0.0625)
-            sig.append(sg)
-        other = [tile([P, N], F32, "other%d" % s) for s in range(PACK)]
-        sm = [tile([P, N], F32, "sm%d" % s) for s in range(PACK)]
-        for s in range(PACK + 1):
-            if s < PACK:
-                nc.vector.tensor_copy(other[s][:], cv_win[s][:].indirect(n5_l[:]))
+            cv_banks.append(bank(N, "cv_bank%d" % s, s))
+            product(cv_banks[s], z_q[s], 0, z2_q, every)
+            cv_win.append(tile([P, WINDOW], F32, "cv_win%d" % s))
+            nc.scalar.activation(cv_win[s][:, 0:N], cv_banks[s][:], ACT.Copy, scale=CV_SCALE)
             if s > 0:
-                nc.vector.scalar_tensor_tensor(sm[s - 1][:], banks[s - 1][:], 0.0625, other[s - 1][:], ALU.mult, ALU.max)
+                cv[s] = tile([P, N], F32, "cv%d" % s)
+                nc.scalar.activation(cv[s][:], cv_banks[s][:], ACT.Copy, scale=CV_SCALE)
+
+        sm = [tile([P, N], F32, "sm%d" % s) for s in range(PACK)]
+        other = tile([P, N], F32, "other")
+        nc.vector.tensor_copy(other[:], cv_win[0][:].indirect(n5_l[:]))
+        nc.vector.scalar_tensor_tensor(sm[0][:], cv_banks[0][:], CV_SCALE, other[:], ALU.mult, ALU.max)
+        for s in range(1, PACK):
+            lead = tile([P, N], F32, "lead%d" % s)
+            nc.vector.tensor_tensor(lead[:], cv_win[s][:].indirect(n5_l[:]), cv[s][:], ALU.subtract)
+            gain = tile([P, N], F32, "gain%d" % s)
+            nc.scalar.activation(gain[:], lead[:], ACT.Relu)
+            nc.gpsimd.tensor_tensor(sm[s][:], gain[:], cv[s][:], ALU.add)
+
+        out_rows = out.rearrange("(c s i) n -> s c i n", s=PACK, i=LINE)
+        res = tile([P, LAST, N], F32, "res", on="gain%d" % LAST)
         for s in range(PACK):
-            ds = tile([P, WIN], F32, "ds%d" % s)
+            gate = tile([P, N], F32, "gate%d" % s)
+            nc.scalar.activation(gate[:], cv_banks[s][:], ACT.Sigmoid, scale=CV_SCALE)
+            ds = tile([P, WINDOW], F32, "ds%d" % s, on=None if s else "cv_win%d" % LAST)
             nc.vector.tensor_copy(ds[:].indirect(n4_l[:]), sm[s][:])
-            res = tile([P, N], F32, "res%d" % s)
-            engine = nc.vector if s == PACK - 1 else nc.gpsimd
-            engine.tensor_tensor(res[:], ds[:, 0:N], sig[s][:], ALU.mult)
-            nc.sync.dma_start(out_v[s], res[:])
+            if s < LAST:
+                nc.gpsimd.tensor_tensor(res[:, s, :], ds[:, 0:N], gate[:], ALU.mult)
+                nc.sync.dma_start(out_rows[s], res[:, s, :])
+            else:
+                for h, queue in enumerate((nc.sync, nc.scalar)):
+                    part = tile([P, N // 2], F32, "part%d" % h)
+                    nc.vector.tensor_tensor(part[:], ds[:, halves[h]], gate[:, halves[h]], ALU.mult)
+                    queue.dma_start(out_rows[s][:, :, halves[h]], part[:])

from contextlib import ExitStack

import concourse.mybir as mybir
from concourse.masks import make_identity

K, T, S, H, N = 512, 2048, 512, 512, 512
FLOPS = 2 * K * S * H + 2 * K * S * N + 2 * S * H * N

F32 = mybir.dt.float32
BF16 = mybir.dt.bfloat16
I32 = mybir.dt.int32
U32 = mybir.dt.uint32
U16 = mybir.dt.uint16
U8 = mybir.dt.uint8
FP8X4 = mybir.dt.float8_e4m3fn_x4
ALU = mybir.AluOpType
ACT = mybir.ActivationFunctionType

P = 128
PACK = 4
RUN = 8
QUADRANT = 32
GROUP = 16
LINE = 4
WINDOW = 1024
PIECE = 128
CV_SCALE = 0.0625
LAST = PACK - 1
TENSOR_TILES = (0, 1)
VECTOR_TILES = (2, 3)


def tile_picked_momtop2sendg_none_p_kernel(
    tc, x_words, x_scales, wa, wb, gt, gi, offs, two, n1, n2, n3, n4, n5, out
):
    nc = tc.nc
    with ExitStack() as ctx:
        sb = ctx.enter_context(tc.tile_pool(name="sb", bufs=1))
        ps = ctx.enter_context(tc.psum_pool(name="ps", bufs=1))

        def tile(shape, dtype, name, on=None):
            return sb.tile(shape, dtype, name=name, tag=on or name, align_bytes=64)

        def bank(width, name, number):
            return ps.tile([P, width], F32, name=name, tag="bank%d" % number)

        def load_list(src, name):
            dst = tile([P, S // GROUP], U16, name)
            nc.sync.dma_start(dst[:], src)
            return dst

        def load_factor(vec, name):
            rows = tile([P, P], F32, name)
            nc.vector.memset(rows[:], 0.0)
            nc.sync.dma_start(
                rows[0:PACK, :].rearrange("t (g e) -> t g e", e=RUN),
                vec.rearrange("(g t e) o -> t g (e o)", t=PACK, e=RUN),
            )
            return rows

        def load_weight(cols, name):
            raw = tile([P, PACK, cols.shape[1]], F32, name)
            nc.sync.dma_start(raw[:], cols.rearrange("(p j) n -> p j n", j=PACK))
            return raw

        zero = tile([P, 1], F32, "zero")
        nc.gpsimd.memset(zero[:], 0.0)
        half = tile([P, 1], F32, "half")
        nc.scalar.activation(half[:], zero[:], ACT.Sigmoid)
        ident = tile([P, P], F32, "ident")
        make_identity(nc, ident[:])

        offs_l = load_list(offs, "offs_l")
        words = tile([P, T], I32, "words")
        nc.sync.dma_start(words[:], x_words[0].rearrange("p c r -> p (c r)").bitcast(I32))
        two_l = load_list(two, "two_l")
        gt_rows = load_factor(gt, "gt_rows")
        scales = tile([P, T], U8, "scales")
        nc.vector.memset(scales[:].bitcast(I32), 0)
        for q in range(P // QUADRANT):
            nc.sync.dma_start(
                scales[QUADRANT * q : QUADRANT * q + PACK, :].bitcast(I32),
                x_scales[0, PACK * q : PACK * (q + 1), :].bitcast(I32),
            )
        halves = [slice(0, H // 2), slice(H // 2, H)]
        wa_raw = [load_weight(wa[:, cols], "wa_raw%d" % h) for h, cols in enumerate(halves)]
        n1_l = load_list(n1, "n1_l")
        n2_l = load_list(n2, "n2_l")
        n3_l = load_list(n3, "n3_l")
        gi_rows = load_factor(gi, "gi_rows")
        wb_raw = load_weight(wb, "wb_raw")
        n5_l = load_list(n5, "n5_l")
        n4_l = load_list(n4, "n4_l")

        def turn_factor(rows, name, number):
            turned_rows = bank(P, name, number)
            nc.tensor.transpose(turned_rows[:], rows[:], ident[:])
            return turned_rows[:, 0:PACK]

        gt_cols = turn_factor(gt_rows, "gt_cols", 4)
        half_gt = tile([P, PACK], F32, "half_gt")
        nc.scalar.activation(half_gt[:], gt_cols, ACT.Abs, scale=0.5)
        sign_or_zero = tile([P, PACK], F32, "sign_or_zero")
        nc.scalar.activation(sign_or_zero[:], gt_cols, ACT.Sign)
        sign_gt = tile([P, PACK], F32, "sign_gt")
        nc.scalar.activation(sign_gt[:], sign_or_zero[:], ACT.Sign, bias=half[:])

        def pick_words(lst, name):
            dealt = tile([P, S], I32, name)
            nc.vector.tensor_copy(
                dealt[:].bitcast(U32).rearrange("p (t g e) -> p g t e", t=PACK, e=RUN),
                words[:].bitcast(U32).indirect(lst[:]),
            )
            return dealt

        def pick_scales(lst, name, on=None):
            plain = tile([P, S], U8, name + "_plain", on)
            nc.vector.tensor_copy(plain[:], scales[:].indirect(lst[:]))
            dealt = tile([P, S], U8, name)
            nc.vector.tensor_copy(
                dealt[:].bitcast(I32).rearrange("p (t g e) -> p g t e", t=PACK, e=RUN // 4),
                plain[:].bitcast(I32).rearrange("p (g t e) -> p g t e", t=PACK, e=RUN // 4),
            )
            return dealt

        def interleave(grouped, raw):
            for c0 in range(0, raw.shape[2], PIECE):
                nc.scalar.copy(
                    grouped[:, c0 : c0 + PIECE, :].rearrange("p (c i) j -> p c j i", i=LINE),
                    raw[:, :, c0 : c0 + PIECE].rearrange("p j (c i) -> p c j i", i=LINE),
                )

        def packed(width, name):
            return tile([P, width], I32, name + "_codes"), tile([P, width], U8, name + "_scales")

        def quantize(operand, cols, grouped):
            nc.vector.quantize_mx(
                operand[0][:, cols].bitcast(FP8X4), operand[1][:, cols], grouped[:].rearrange("p c j -> p (c j)")
            )

        def product(result, lhs, t, rhs, cols):
            lhs_cols = slice(P * t, P * (t + 1))
            nc.tensor.matmul_mx(
                result[:],
                lhsT=lhs[0][:, lhs_cols].bitcast(FP8X4),
                lhsT_scale=lhs[1][:, lhs_cols],
                rhs=rhs[0][:, cols].bitcast(FP8X4),
                rhs_scale=rhs[1][:, cols],
                start=True,
                stop=True,
            )

        every = slice(0, N)
        xa_words = pick_words(offs_l, "xa_words")
        xb_words = pick_words(two_l, "xb_words")
        xa = (xa_words, pick_scales(offs_l, "xa_scales"))
        wa_q = packed(H, "wa")
        a_win = [tile([P, WINDOW], F32, "a_win%d" % t) for t in range(PACK)]
        for h, cols in enumerate(halves):
            wa_grouped = tile([P, H // 2, PACK], BF16, "wa_grouped%d" % h)
            interleave(wa_grouped, wa_raw[h])
            quantize(wa_q, cols, wa_grouped)
            a_half = bank(H // 2, "a_half%d" % h, 6 + h)
            product(a_half, xa, 0, wa_q, cols)
            nc.scalar.activation(a_win[0][:, cols], a_half[:], ACT.Copy, scale=half_gt[:, 0:1])
        xb = (xb_words, pick_scales(two_l, "xb_scales", on="wa_grouped1"))
        for t in range(1, PACK):
            a_bank = bank(H, "a_bank%d" % t, t)
            product(a_bank, xa, t, wa_q, every)
            nc.scalar.activation(a_win[t][:, 0:H], a_bank[:], ACT.Copy, scale=half_gt[:, t : t + 1])

        gi_cols = turn_factor(gi_rows, "gi_cols", 5)
        signed_gi = tile([P, PACK], F32, "signed_gi")
        nc.vector.tensor_tensor(signed_gi[:], gi_cols, sign_gt[:], ALU.mult)
        wb_grouped = tile([P, N, PACK], BF16, "wb_grouped")
        interleave(wb_grouped, wb_raw)

        hi = tile([P, PACK, H], F32, "hi")
        rest = tile([P, PACK, H], F32, "rest")
        b1 = [tile([P, H], F32, "b1_%d" % t) for t in range(PACK)]
        diff = [tile([P, H], F32, "diff_%d" % t) for t in range(PACK)]
        gap = [tile([P, H], F32, "gap_%d" % t) for t in range(PACK)]
        over = [tile([P, H], F32, "over_%d" % t) for t in range(PACK)]
        under = [tile([P, H], F32, "under_%d" % t) for t in range(PACK)]

        def look_up(pair):
            for t in pair:
                nc.vector.tensor_copy(b1[t][:], a_win[t][:].indirect(n1_l[:]))
            for t in pair:
                nc.vector.tensor_tensor(diff[t][:], a_win[t][:].indirect(n2_l[:]), b1[t][:], ALU.subtract)
                nc.scalar.activation(gap[t][:], diff[t][:], ACT.Abs)
            for t in pair:
                nc.vector.scalar_tensor_tensor(hi[:, t, :], diff[t][:], 0.0, b1[t][:], ALU.max, ALU.add)
            for t in pair:
                nc.vector.tensor_tensor(over[t][:], a_win[t][:].indirect(n3_l[:]), hi[:, t, :], ALU.subtract)
            for t in pair:
                nc.vector.scalar_tensor_tensor(under[t][:], over[t][:], -1.0, gap[t][:], ALU.mult, ALU.min)

        z_rows = tile([P, PACK, H], BF16, "z_rows")

        def sum_turned(pair):
            up = {t: tile([P, H], F32, "up_%d" % t) for t in pair}
            down = {t: tile([P, H], F32, "down_%d" % t) for t in pair}
            for t in pair:
                nc.scalar.activation(up[t][:], over[t][:], ACT.Relu, scale=2.0)
            for t in pair:
                nc.scalar.activation(down[t][:], under[t][:], ACT.Relu)
            sums = {}
            for t in pair:
                sum_bank = bank(H, "sum_bank%d" % t, t)
                for c0 in range(0, H, P):
                    cols = slice(c0, c0 + P)
                    terms = (hi[:, t, cols], up[t][:, cols], down[t][:, cols])
                    for i, term in enumerate(terms):
                        nc.tensor.matmul(
                            sum_bank[:, cols], term, ident[:], is_transpose=True, start=i == 0, stop=i == len(terms) - 1
                        )
                sums[t] = tile([P, H], F32, "sum_%d" % t)
                nc.scalar.copy(sums[t][:], sum_bank[:])
            return sums

        def turn_back(sums):
            for t in sums:
                back_bank = bank(H, "back_bank%d" % t, t + len(sums))
                for c0 in range(0, H, P):
                    cols = slice(c0, c0 + P)
                    nc.tensor.transpose(back_bank[:, cols], sums[t][:, cols], ident[:])
                nc.scalar.copy(z_rows[:, t, :], back_bank[:])

        def sum_plain(pair):
            for t in pair:
                nc.vector.scalar_tensor_tensor(rest[:, t, :], over[t][:], 2.0, under[t][:], ALU.mult, ALU.max)
            for t in pair:
                nc.vector.tensor_tensor(z_rows[:, t, :], hi[:, t, :], rest[:, t, :], ALU.add)

        look_up(TENSOR_TILES)
        turned_sums = sum_turned(TENSOR_TILES)
        wb_q = packed(N, "wb")
        quantize(wb_q, every, wb_grouped)
        z2_rows = tile([P, PACK, N], BF16, "z2_rows")
        for t in range(PACK):
            b_bank = bank(N, "b_bank%d" % t, PACK + t)
            product(b_bank, xb, t, wb_q, every)
            nc.scalar.activation(z2_rows[:, t, :], b_bank[:], ACT.Copy, scale=signed_gi[:, t : t + 1])
        look_up(VECTOR_TILES)
        turn_back(turned_sums)
        z2_grouped = tile([P, N, PACK], BF16, "z2_grouped")
        interleave(z2_grouped, z2_rows)
        z2_q = packed(N, "z2")
        quantize(z2_q, every, z2_grouped)
        sum_plain(VECTOR_TILES)

        z_dealt = z_rows[:].rearrange("p t (c s i) -> p s c t i", s=PACK, i=LINE)
        z_grouped = [tile([P, P, PACK], BF16, "z_grouped%d" % s) for s in range(PACK)]
        for s in range(PACK):
            copy = nc.scalar.copy if s % 2 else nc.vector.tensor_copy
            copy(z_grouped[s][:].rearrange("p (c i) t -> p c t i", i=LINE), z_dealt[:, s])
        z_q = []
        for s in range(PACK):
            z_q.append(packed(P, "z_tile%d" % s))
            quantize(z_q[s], slice(0, P), z_grouped[s])

        cv_banks, cv_win, cv = [], [], {}
        for s in range(PACK):
            cv_banks.append(bank(N, "cv_bank%d" % s, s))
            product(cv_banks[s], z_q[s], 0, z2_q, every)
            cv_win.append(tile([P, WINDOW], F32, "cv_win%d" % s))
            nc.scalar.activation(cv_win[s][:, 0:N], cv_banks[s][:], ACT.Copy, scale=CV_SCALE)
            if s > 0:
                cv[s] = tile([P, N], F32, "cv%d" % s)
                nc.scalar.activation(cv[s][:], cv_banks[s][:], ACT.Copy, scale=CV_SCALE)

        sm = [tile([P, N], F32, "sm%d" % s) for s in range(PACK)]
        other = tile([P, N], F32, "other")
        nc.vector.tensor_copy(other[:], cv_win[0][:].indirect(n5_l[:]))
        nc.vector.scalar_tensor_tensor(sm[0][:], cv_banks[0][:], CV_SCALE, other[:], ALU.mult, ALU.max)
        for s in range(1, PACK):
            lead = tile([P, N], F32, "lead%d" % s)
            nc.vector.tensor_tensor(lead[:], cv_win[s][:].indirect(n5_l[:]), cv[s][:], ALU.subtract)
            gain = tile([P, N], F32, "gain%d" % s)
            nc.scalar.activation(gain[:], lead[:], ACT.Relu)
            nc.gpsimd.tensor_tensor(sm[s][:], gain[:], cv[s][:], ALU.add)

        out_rows = out.rearrange("(c s i) n -> s c i n", s=PACK, i=LINE)
        res = tile([P, LAST, N], F32, "res", on="gain%d" % LAST)
        for s in range(PACK):
            gate = tile([P, N], F32, "gate%d" % s)
            nc.scalar.activation(gate[:], cv_banks[s][:], ACT.Sigmoid, scale=CV_SCALE)
            ds = tile([P, WINDOW], F32, "ds%d" % s, on=None if s else "cv_win%d" % LAST)
            nc.vector.tensor_copy(ds[:].indirect(n4_l[:]), sm[s][:])
            if s < LAST:
                nc.gpsimd.tensor_tensor(res[:, s, :], ds[:, 0:N], gate[:], ALU.mult)
                nc.sync.dma_start(out_rows[s], res[:, s, :])
            else:
                for h, queue in enumerate((nc.sync, nc.scalar)):
                    part = tile([P, N // 2], F32, "part%d" % h)
                    nc.vector.tensor_tensor(part[:], ds[:, halves[h]], gate[:, halves[h]], ALU.mult)
                    queue.dma_start(out_rows[s][:, :, halves[h]], part[:])
